import numpy as np
import ml_dtypes


def mxq(x, axis, fmt="e4m3"):
    dtype, down = {"e4m3": (ml_dtypes.float8_e4m3fn, 7), "e5m2": (ml_dtypes.float8_e5m2, 14)}[fmt]
    v = np.moveaxis(np.asarray(x, np.float32).astype(ml_dtypes.bfloat16).astype(np.float64), axis, -1)
    blocks = v.reshape(v.shape[:-1] + (-1, 32))
    amax = np.abs(blocks).max(-1, keepdims=True)
    byte = np.maximum(np.where(amax > 0, np.frexp(amax)[1] - 1 + 127, 0) - down, 1)
    scale = np.exp2(byte - 127.0)
    codes = (blocks / scale).astype(np.float32).astype(dtype).astype(np.float64)
    return np.moveaxis((codes * scale).reshape(v.shape), -1, axis)


WIDE = False


def mx_kscale(k):
    if not WIDE:
        return np.ones(k)
    levels = np.array([10, -10, 5, -5, 0])
    if k % 512:
        return np.exp2(np.random.permutation(np.resize(levels, k // 32))).repeat(32)
    a = np.empty((k // 512, 16))
    for p in range(k // 512):
        a[p, :8] = np.random.permutation(np.resize(levels, 8))
        for g in range(8):
            far = levels[np.abs(levels - a[p, g]) >= 10]
            a[p, g + 8] = far[np.random.randint(len(far))]
    return np.exp2(a.ravel()).repeat(32)


def f64(x):
    return np.asarray(x).astype(np.float64)


def striped(idx):
    return np.tile(idx.reshape(-1, 16).T, (8, 1)).astype(np.uint16)


def unstriped(offs):
    return offs[:16].T.reshape(-1).astype(np.int64)


K, T, E, C, N = 1536, 512, 4, 256, 512


def by_expert(wq, xq):
    return np.concatenate([wq[e].T @ xq[:, e * C:(e + 1) * C] for e in range(E)], axis=1)


def setup_inputs():
    n = np.random.standard_normal
    s = mx_kscale(K)[:, None]
    first = np.random.permutation(np.repeat(np.arange(E), T // E))
    second = (first + 1 + np.random.permutation(np.repeat(np.arange(E - 1), -(-T // (E - 1)))[:T])) % E
    while np.bincount(second, minlength=E).max() != T // E:
        load = np.bincount(second, minlength=E); hi, lo = int(load.argmax()), int(load.argmin())
        t = np.flatnonzero((second == hi) & (first != lo))[0]; second[t] = lo
    slot_token = np.empty(E * C, np.int64); pos = np.empty((2, T), np.int64); fill = np.zeros(E, np.int64)
    place = np.stack([np.random.permutation(C) for _ in range(E)])
    for r, deal in enumerate((first, second)):
        for t in np.random.permutation(T):
            e = deal[t]; j = e * C + place[e, fill[e]]; fill[e] += 1; slot_token[j] = t; pos[r, t] = j
    g = np.random.uniform(0.2, 0.8, T)
    return {
        "xT": (n((K, T)) * s).astype(np.float32),
        "w": (n((E, K, N)) / np.sqrt(K) / s[None]).astype(np.float32),
        "b": (0.3 * n((N, E))).astype(np.float32),
        "gate": np.stack([np.tile(g, (N, 1)), np.tile(1.0 - g, (N, 1))]).astype(np.float32),
        "offs": striped(slot_token),
        "pos1": striped(pos[0]),
        "pos2": striped(pos[1]),
    }


def reference(xT, w, b, gate, offs, pos1, pos2):
    idx = unstriped(offs)
    xq = mxq(f64(xT)[:, idx], 0, "e4m3")
    y = by_expert(mxq(f64(w), 1, "e4m3"), xq)
    y = y + np.repeat(f64(b), C, axis=1)
    return f64(gate[0]) * y[:, unstriped(pos1)] + f64(gate[1]) * y[:, unstriped(pos2)]

@@ -1,0 +1,169 @@
+from contextlib import ExitStack
+
+import concourse.mybir as mybir
+from concourse.masks import make_identity
+
+K, T, E, C, N = 1536, 512, 4, 256, 512
+FLOPS = 2 * K * N * E * C
+
+F32 = mybir.dt.float32
+BF16 = mybir.dt.bfloat16
+U32 = mybir.dt.uint32
+U16 = mybir.dt.uint16
+U8 = mybir.dt.uint8
+FP8X4 = mybir.dt.float8_e4m3fn_x4
+MULT = mybir.AluOpType.mult
+ADD = mybir.AluOpType.add
+IDENTITY = mybir.ActivationFunctionType.Identity
+
+P = 128
+PACK = 4
+K_PASS = P * PACK
+PASSES = K // K_PASS
+SLOTS = E * C
+BLOCKS = N // P
+GATHER_CUTS = ((0, 384), (384, 768), (768, 1024))
+X_VECTOR = (320, 0, 0)
+
+CHUNKS = (
+    (0, 0, 512, (0, 0, 0)), (1, 0, 512, (0, 512, 0)),
+    (2, 0, 256, (0, 256, 0)), (3, 0, 256, (0, 256, 0)),
+    (2, 256, 256, (0, 256, 0)), (3, 256, 128, (0, 128, 0)), (3, 384, 128, (0, 128, 64)),
+)
+RAW_BUFS = {512: 8, 256: 7, 128: 6}
+GROUPED_BUFS = {512: 5, 256: 4, 128: 3}
+CODES_BUFS = {512: 4, 256: 6, 128: 4}
+
+
+def tile_routed_moe_kernel(tc, xT, w, b, gate, offs, pos1, pos2, out):
+    nc = tc.nc
+    with ExitStack() as ctx:
+        keep = ctx.enter_context(tc.tile_pool(name="keep", bufs=1))
+        stage = ctx.enter_context(tc.tile_pool(name="stage", bufs=2))
+        psum = ctx.enter_context(tc.psum_pool(name="psum", bufs=6))
+
+        offs_sb = keep.tile([P, SLOTS // 16], U16, name="offs_sb")
+        pos1_sb = keep.tile([P, T // 16], U16, name="pos1_sb")
+        pos2_sb = keep.tile([P, T // 16], U16, name="pos2_sb")
+        bias = keep.tile([P, BLOCKS, E], F32, name="bias")
+        x_scales = keep.tile([P, T], U8, name="x_scales", align_bytes=64)
+        g_scales = keep.tile([P, SLOTS], U8, name="g_scales", align_bytes=64)
+        y = [keep.tile([P, SLOTS], F32, name="y%d" % i) for i in range(BLOCKS)]
+        gates = [keep.tile([P, 2, 2, T], F32, name="gates%d" % i) for i in range(2)]
+
+        nc.gpsimd.memset(x_scales[:], 0)
+        ident = keep.tile([P, P], F32, name="ident")
+        make_identity(nc, ident[:])
+
+        x_raw = []
+        for g in range(PASSES):
+            raw = stage.tile([P, PACK, 512], F32, name="raw512", bufs=RAW_BUFS[512])
+            nc.sync.dma_start(raw[:], xT[g * K_PASS:(g + 1) * K_PASS, :].rearrange("(p j) t -> p j t", j=PACK))
+            x_raw.append(raw)
+            if g == 0:
+                nc.sync.dma_start(offs_sb[:], offs)
+        nc.scalar.dma_start(bias[:], b.rearrange("(c p) e -> p c e", p=P))
+
+        def load_w(chunk):
+            e, c0, width, on_vector = chunk
+            raws = []
+            for g in range(PASSES):
+                raw = stage.tile([P, PACK, width], F32, name="raw%d" % width, bufs=RAW_BUFS[width])
+                nc.sync.dma_start(
+                    raw[:], w[e, g * K_PASS:(g + 1) * K_PASS, c0:c0 + width].rearrange("(p j) n -> p j n", j=PACK))
+                raws.append(raw)
+            return raws
+
+        def load_gates(h):
+            for k in range(2):
+                nc.sync.dma_start(
+                    gates[h][:, k, :, :], gate[k, h * 256:(h + 1) * 256, :].rearrange("(c p) t -> p c t", p=P))
+
+        def interleave(dst, raw, width, on_vector):
+            cut = width - on_vector
+            if cut > 0:
+                nc.scalar.copy(dst[:, 0:cut, :], raw[:, :, 0:cut].rearrange("p j c -> p c j"))
+            if on_vector > 0:
+                nc.vector.tensor_copy(dst[:, cut:width, :], raw[:, :, cut:width].rearrange("p j c -> p c j"))
+
+        w_raw = {}
+        w_raw[CHUNKS[0]] = load_w(CHUNKS[0])
+        nc.sync.dma_start(pos1_sb[:], pos1)
+        nc.sync.dma_start(pos2_sb[:], pos2)
+
+        x_codes = []
+        g_codes = []
+        for g in range(PASSES):
+            grouped = stage.tile([P, T, PACK], BF16, name="x_grouped", bufs=2, align_bytes=64)
+            interleave(grouped, x_raw[g], T, X_VECTOR[g])
+            codes = keep.tile([P, T], U32, name="x_codes%d" % g, align_bytes=64)
+            nc.vector.quantize_mx(
+                out=codes[:].bitcast(FP8X4), scales=x_scales[4 * g:P, :],
+                in_=grouped[:].rearrange("p t j -> p (t j)"))
+            x_codes.append(codes)
+            g_codes.append(keep.tile([P, SLOTS], U32, name="g_codes%d" % g, align_bytes=64))
+            for s0, s1 in GATHER_CUTS:
+                nc.vector.tensor_copy(g_codes[g][:, s0:s1], x_codes[g][:].indirect(offs_sb[:, s0 // 16:s1 // 16]))
+        for s0, s1 in GATHER_CUTS:
+            nc.vector.tensor_copy(g_scales[:, s0:s1], x_scales[:].indirect(offs_sb[:, s0 // 16:s1 // 16]))
+
+        def run_chunk(chunk, raws, last):
+            e, c0, width, on_vector = chunk
+            blocks = range(c0 // P, (c0 + width) // P)
+            slots = slice(e * C, (e + 1) * C)
+            accs = {}
+            for g in range(PASSES):
+                grouped = stage.tile(
+                    [P, width, PACK], BF16, name="w_grouped%d" % width, bufs=GROUPED_BUFS[width], align_bytes=64)
+                interleave(grouped, raws[g], width, on_vector[g])
+                codes = stage.tile([P, width], U32, name="w_codes%d" % width, bufs=CODES_BUFS[width], align_bytes=64)
+                scales = stage.tile([P, width], U8, name="w_scales%d" % width, bufs=CODES_BUFS[width], align_bytes=64)
+                nc.vector.quantize_mx(
+                    out=codes[:].bitcast(FP8X4), scales=scales[:], in_=grouped[:].rearrange("p n j -> p (n j)"))
+                for i in blocks:
+                    if g == 0:
+                        accs[i] = psum.tile([P, C], F32, name="acc")
+                    cols = slice(i * P - c0, (i + 1) * P - c0)
+                    nc.tensor.matmul_mx(
+                        out=accs[i][:],
+                        lhsT=codes[:, cols].bitcast(FP8X4), lhsT_scale=scales[:, cols],
+                        rhs=g_codes[g][:, slots].bitcast(FP8X4), rhs_scale=g_scales[4 * g:P, slots],
+                        start=(g == 0), stop=(g == PASSES - 1))
+            for i in blocks:
+                if last and i % 2 == 1:
+                    nc.vector.tensor_scalar(y[i][:, slots], accs[i][:], bias[:, i, e:e + 1], None, ADD)
+                else:
+                    nc.scalar.activation(y[i][:, slots], accs[i][:], IDENTITY, bias=bias[:, i, e:e + 1])
+
+        def combine(i, pieces):
+            size = T // pieces
+            for q in range(pieces):
+                t = slice(q * size, (q + 1) * size)
+                o = slice(q * size // 16, (q + 1) * size // 16)
+                first = stage.tile([P, size], F32, name="first%d" % size, bufs=2)
+                second = stage.tile([P, size], F32, name="second%d" % size, bufs=2)
+                nc.vector.tensor_tensor(first[:], y[i][:].indirect(pos1_sb[:, o]), gates[i // 2][:, 0, i % 2, t], MULT)
+                nc.vector.tensor_tensor(second[:], y[i][:].indirect(pos2_sb[:, o]), gates[i // 2][:, 1, i % 2, t], MULT)
+                if pieces == 1:
+                    total = psum.tile([P, T], F32, name="total", bufs=2)
+                    nc.tensor.matmul(total[:], ident[:], first[:], start=True, stop=False)
+                    nc.tensor.matmul(total[:], ident[:], second[:], start=False, stop=True)
+                    result = stage.tile([P, T], F32, name="result", bufs=2)
+                    nc.scalar.copy(result[:], total[:])
+                    nc.sync.dma_start(out[i * P:(i + 1) * P, t], result[:])
+                    continue
+                nc.vector.tensor_tensor(first[:], first[:], second[:], ADD)
+                nc.sync.dma_start(out[i * P:(i + 1) * P, t], first[:])
+
+        for position, chunk in enumerate(CHUNKS[1:]):
+            w_raw[chunk] = load_w(chunk)
+            if position == 2:
+                load_gates(0)
+            if position == 4:
+                load_gates(1)
+        for chunk in CHUNKS:
+            run_chunk(chunk, w_raw[chunk], False)
+        combine(0, 1)
+        combine(1, 1)
+        combine(2, 1)
+        combine(3, 2)

@@ -28,7 +28,7 @@ X_VECTOR = (320, 0, 0)
 CHUNKS = (
     (0, 0, 512, (0, 0, 0)), (1, 0, 512, (0, 512, 0)),
     (2, 0, 256, (0, 256, 0)), (3, 0, 256, (0, 256, 0)),
-    (2, 256, 256, (0, 256, 0)), (3, 256, 128, (0, 128, 0)), (3, 384, 128, (0, 128, 64)),
+    (2, 256, 256, (0, 0, 0)), (3, 256, 128, (0, 0, 0)), (3, 384, 128, (0, 0, 64)),
 )
 RAW_BUFS = {512: 8, 256: 7, 128: 6}
 GROUPED_BUFS = {512: 5, 256: 4, 128: 3}
@@ -157,13 +157,15 @@ def tile_routed_moe_kernel(tc, xT, w, b, gate, offs, pos1, pos2, out):
 
         for position, chunk in enumerate(CHUNKS[1:]):
             w_raw[chunk] = load_w(chunk)
-            if position == 2:
+            if position == 0:
                 load_gates(0)
-            if position == 4:
+            if position == 3:
                 load_gates(1)
-        for chunk in CHUNKS:
+        for position, chunk in enumerate(CHUNKS):
             run_chunk(chunk, w_raw[chunk], False)
-        combine(0, 1)
-        combine(1, 1)
-        combine(2, 1)
+            if position == 3:
+                combine(0, 1)
+                combine(1, 1)
+            if position == 5:
+                combine(2, 1)
         combine(3, 2)

@@ -14,7 +14,6 @@ U8 = mybir.dt.uint8
 FP8X4 = mybir.dt.float8_e4m3fn_x4
 MULT = mybir.AluOpType.mult
 ADD = mybir.AluOpType.add
-IDENTITY = mybir.ActivationFunctionType.Identity
 
 P = 128
 PACK = 4
@@ -25,14 +24,18 @@ BLOCKS = N // P
 GATHER_CUTS = ((0, 384), (384, 768), (768, 1024))
 X_VECTOR = (320, 0, 0)
 
+PAIR = ((0, 1), (2,))
+EACH = ((0,), (1,), (2,))
 CHUNKS = (
-    (0, 0, 512, (0, 0, 0)), (1, 0, 512, (0, 512, 0)),
-    (2, 0, 256, (0, 256, 0)), (3, 0, 256, (0, 256, 0)),
-    (2, 256, 256, (0, 0, 0)), (3, 256, 128, (0, 0, 0)), (3, 384, 128, (0, 0, 64)),
+    (0, 0, 512, ((0, 0), (0, 0), (0, 0)), PAIR),
+    (1, 0, 512, ((0, 0), (512, 0), (0, 0)), EACH),
+    (2, 0, 512, ((0, 0), (512, 0), (0, 0)), EACH),
+    (3, 0, 256, ((0, 0), (0, 0), (0, 0)), EACH),
+    (3, 256, 256, ((0, 0), (0, 0), (128, 0)), EACH),
 )
-RAW_BUFS = {512: 8, 256: 7, 128: 6}
-GROUPED_BUFS = {512: 5, 256: 4, 128: 3}
-CODES_BUFS = {512: 4, 256: 6, 128: 4}
+RAW_BUFS = {512: 12, 256: 6}
+GROUPED_BUFS = {1024: 1, 512: 5, 256: 3}
+CODES_BUFS = {1024: 1, 512: 4, 256: 4}
 
 
 def tile_routed_moe_kernel(tc, xT, w, b, gate, offs, pos1, pos2, out):
@@ -40,7 +43,7 @@ def tile_routed_moe_kernel(tc, xT, w, b, gate, offs, pos1, pos2, out):
     with ExitStack() as ctx:
         keep = ctx.enter_context(tc.tile_pool(name="keep", bufs=1))
         stage = ctx.enter_context(tc.tile_pool(name="stage", bufs=2))
-        psum = ctx.enter_context(tc.psum_pool(name="psum", bufs=6))
+        psum = ctx.enter_context(tc.psum_pool(name="psum", bufs=8))
 
         offs_sb = keep.tile([P, SLOTS // 16], U16, name="offs_sb")
         pos1_sb = keep.tile([P, T // 16], U16, name="pos1_sb")
@@ -50,9 +53,9 @@ def tile_routed_moe_kernel(tc, xT, w, b, gate, offs, pos1, pos2, out):
         g_scales = keep.tile([P, SLOTS], U8, name="g_scales", align_bytes=64)
         y = [keep.tile([P, SLOTS], F32, name="y%d" % i) for i in range(BLOCKS)]
         gates = [keep.tile([P, 2, 2, T], F32, name="gates%d" % i) for i in range(2)]
+        ident = keep.tile([P, P], F32, name="ident")
 
         nc.gpsimd.memset(x_scales[:], 0)
-        ident = keep.tile([P, P], F32, name="ident")
         make_identity(nc, ident[:])
 
         x_raw = []
@@ -65,7 +68,7 @@ def tile_routed_moe_kernel(tc, xT, w, b, gate, offs, pos1, pos2, out):
         nc.scalar.dma_start(bias[:], b.rearrange("(c p) e -> p c e", p=P))
 
         def load_w(chunk):
-            e, c0, width, on_vector = chunk
+            e, c0, width = chunk[:3]
             raws = []
             for g in range(PASSES):
                 raw = stage.tile([P, PACK, width], F32, name="raw%d" % width, bufs=RAW_BUFS[width])
@@ -79,23 +82,28 @@ def tile_routed_moe_kernel(tc, xT, w, b, gate, offs, pos1, pos2, out):
                 nc.sync.dma_start(
                     gates[h][:, k, :, :], gate[k, h * 256:(h + 1) * 256, :].rearrange("(c p) t -> p c t", p=P))
 
-        def interleave(dst, raw, width, on_vector):
-            cut = width - on_vector
-            if cut > 0:
-                nc.scalar.copy(dst[:, 0:cut, :], raw[:, :, 0:cut].rearrange("p j c -> p c j"))
-            if on_vector > 0:
-                nc.vector.tensor_copy(dst[:, cut:width, :], raw[:, :, cut:width].rearrange("p j c -> p c j"))
+        def interleave(dst, raw, width, on_vector, on_gpsimd):
+            first = width - on_vector - on_gpsimd
+            second = width - on_gpsimd
+            for copy, c0, c1 in ((nc.scalar.copy, 0, first), (nc.vector.tensor_copy, first, second)):
+                if c1 > c0:
+                    copy(
+                        dst[:, c0:c1, :].rearrange("p (c i) j -> p c j i", i=4),
+                        raw[:, :, c0:c1].rearrange("p j (c i) -> p c j i", i=4))
+            if on_gpsimd > 0:
+                nc.gpsimd.tensor_scalar(
+                    dst[:, second:width, :].rearrange("p (c i) j -> p c j i", i=4),
+                    raw[:, :, second:width].rearrange("p j (c i) -> p c j i", i=4), 1.0, 0.0, MULT, ADD)
 
-        w_raw = {}
-        w_raw[CHUNKS[0]] = load_w(CHUNKS[0])
+        w_raw = [load_w(CHUNKS[0])]
         nc.sync.dma_start(pos1_sb[:], pos1)
         nc.sync.dma_start(pos2_sb[:], pos2)
 
         x_codes = []
         g_codes = []
         for g in range(PASSES):
-            grouped = stage.tile([P, T, PACK], BF16, name="x_grouped", bufs=2, align_bytes=64)
-            interleave(grouped, x_raw[g], T, X_VECTOR[g])
+            grouped = stage.tile([P, T, PACK], BF16, name="w_grouped512", bufs=GROUPED_BUFS[512], align_bytes=64)
+            interleave(grouped, x_raw[g], T, X_VECTOR[g], 0)
             codes = keep.tile([P, T], U32, name="x_codes%d" % g, align_bytes=64)
             nc.vector.quantize_mx(
                 out=codes[:].bitcast(FP8X4), scales=x_scales[4 * g:P, :],
@@ -107,65 +115,71 @@ def tile_routed_moe_kernel(tc, xT, w, b, gate, offs, pos1, pos2, out):
         for s0, s1 in GATHER_CUTS:
             nc.vector.tensor_copy(g_scales[:, s0:s1], x_scales[:].indirect(offs_sb[:, s0 // 16:s1 // 16]))
 
-        def run_chunk(chunk, raws, last):
-            e, c0, width, on_vector = chunk
+        accs = {}
+
+        def run_chunk(chunk, raws):
+            e, c0, width, shares, groups = chunk
             blocks = range(c0 // P, (c0 + width) // P)
             slots = slice(e * C, (e + 1) * C)
-            accs = {}
-            for g in range(PASSES):
+            for group in groups:
+                columns = len(group) * width
                 grouped = stage.tile(
-                    [P, width, PACK], BF16, name="w_grouped%d" % width, bufs=GROUPED_BUFS[width], align_bytes=64)
-                interleave(grouped, raws[g], width, on_vector[g])
-                codes = stage.tile([P, width], U32, name="w_codes%d" % width, bufs=CODES_BUFS[width], align_bytes=64)
-                scales = stage.tile([P, width], U8, name="w_scales%d" % width, bufs=CODES_BUFS[width], align_bytes=64)
+                    [P, columns, PACK], BF16, name="w_grouped%d" % columns, bufs=GROUPED_BUFS[columns], align_bytes=64)
+                codes = stage.tile(
+                    [P, columns], U32, name="w_codes%d" % columns, bufs=CODES_BUFS[columns], align_bytes=64)
+                scales = stage.tile(
+                    [P, columns], U8, name="w_scales%d" % columns, bufs=CODES_BUFS[columns], align_bytes=64)
+                for r, g in enumerate(group):
+                    interleave(grouped[:, r * width:(r + 1) * width, :], raws[g], width, shares[g][0], shares[g][1])
                 nc.vector.quantize_mx(
                     out=codes[:].bitcast(FP8X4), scales=scales[:], in_=grouped[:].rearrange("p n j -> p (n j)"))
-                for i in blocks:
-                    if g == 0:
-                        accs[i] = psum.tile([P, C], F32, name="acc")
-                    cols = slice(i * P - c0, (i + 1) * P - c0)
-                    nc.tensor.matmul_mx(
-                        out=accs[i][:],
-                        lhsT=codes[:, cols].bitcast(FP8X4), lhsT_scale=scales[:, cols],
-                        rhs=g_codes[g][:, slots].bitcast(FP8X4), rhs_scale=g_scales[4 * g:P, slots],
-                        start=(g == 0), stop=(g == PASSES - 1))
-            for i in blocks:
-                if last and i % 2 == 1:
-                    nc.vector.tensor_scalar(y[i][:, slots], accs[i][:], bias[:, i, e:e + 1], None, ADD)
-                else:
-                    nc.scalar.activation(y[i][:, slots], accs[i][:], IDENTITY, bias=bias[:, i, e:e + 1])
+                for r, g in enumerate(group):
+                    for i in blocks:
+                        if g == 0 and e % 2 == 0:
+                            accs[e // 2, i] = psum.tile([P, 2, C], F32, name="acc")
+                        n0 = r * width + i * P - c0
+                        nc.tensor.matmul_mx(
+                            out=accs[e // 2, i][:, e % 2, :],
+                            lhsT=codes[:, n0:n0 + P].bitcast(FP8X4), lhsT_scale=scales[:, n0:n0 + P],
+                            rhs=g_codes[g][:, slots].bitcast(FP8X4), rhs_scale=g_scales[4 * g:P, slots],
+                            start=(g == 0), stop=(g == PASSES - 1))
 
-        def combine(i, pieces):
-            size = T // pieces
-            for q in range(pieces):
-                t = slice(q * size, (q + 1) * size)
-                o = slice(q * size // 16, (q + 1) * size // 16)
-                first = stage.tile([P, size], F32, name="first%d" % size, bufs=2)
-                second = stage.tile([P, size], F32, name="second%d" % size, bufs=2)
-                nc.vector.tensor_tensor(first[:], y[i][:].indirect(pos1_sb[:, o]), gates[i // 2][:, 0, i % 2, t], MULT)
-                nc.vector.tensor_tensor(second[:], y[i][:].indirect(pos2_sb[:, o]), gates[i // 2][:, 1, i % 2, t], MULT)
-                if pieces == 1:
-                    total = psum.tile([P, T], F32, name="total", bufs=2)
-                    nc.tensor.matmul(total[:], ident[:], first[:], start=True, stop=False)
-                    nc.tensor.matmul(total[:], ident[:], second[:], start=False, stop=True)
-                    result = stage.tile([P, T], F32, name="result", bufs=2)
-                    nc.scalar.copy(result[:], total[:])
-                    nc.sync.dma_start(out[i * P:(i + 1) * P, t], result[:])
-                    continue
-                nc.vector.tensor_tensor(first[:], first[:], second[:], ADD)
-                nc.sync.dma_start(out[i * P:(i + 1) * P, t], first[:])
+        def empty(pair, i):
+            nc.vector.tensor_tensor(
+                y[i][:, pair * 2 * C:(pair + 1) * 2 * C].rearrange("p (e c) -> p e c", e=2), accs[pair, i][:],
+                bias[:, i, 2 * pair:2 * pair + 2].unsqueeze(2).to_broadcast([P, 2, C]), ADD)
 
-        for position, chunk in enumerate(CHUNKS[1:]):
-            w_raw[chunk] = load_w(chunk)
-            if position == 0:
-                load_gates(0)
-            if position == 3:
-                load_gates(1)
+        def combine(i):
+            first = stage.tile([P, T], F32, name="first", bufs=2)
+            second = stage.tile([P, T], F32, name="second", bufs=2)
+            nc.vector.tensor_tensor(first[:], y[i][:].indirect(pos1_sb[:]), gates[i // 2][:, 0, i % 2, :], MULT)
+            nc.vector.tensor_tensor(second[:], y[i][:].indirect(pos2_sb[:]), gates[i // 2][:, 1, i % 2, :], MULT)
+            result = stage.tile([P, T], F32, name="result", bufs=2)
+            if i == BLOCKS - 1:
+                nc.vector.tensor_tensor(result[:], first[:], second[:], ADD)
+            else:
+                acc = psum.tile([P, 2, C], F32, name="acc")
+                total = acc[:].rearrange("p e c -> p (e c)")
+                nc.tensor.matmul(total, ident[:], first[:], start=True, stop=False)
+                nc.tensor.matmul(total, ident[:], second[:], start=False, stop=True)
+                nc.scalar.copy(result[:], total)
+            nc.sync.dma_start(out[i * P:(i + 1) * P, :], result[:])
+
+        w_raw += [load_w(chunk) for chunk in CHUNKS[1:4]]
+        load_gates(0)
+        w_raw += [load_w(chunk) for chunk in CHUNKS[4:]]
+        load_gates(1)
         for position, chunk in enumerate(CHUNKS):
-            run_chunk(chunk, w_raw[chunk], False)
+            run_chunk(chunk, w_raw[position])
+            if position == 2:
+                for i in range(BLOCKS):
+                    empty(0, i)
             if position == 3:
-                combine(0, 1)
-                combine(1, 1)
-            if position == 5:
-                combine(2, 1)
-        combine(3, 2)
+                empty(1, 0)
+                empty(1, 1)
+                combine(0)
+        combine(1)
+        empty(1, 2)
+        empty(1, 3)
+        combine(2)
+        combine(3)

@@ -14,6 +14,7 @@ U8 = mybir.dt.uint8
 FP8X4 = mybir.dt.float8_e4m3fn_x4
 MULT = mybir.AluOpType.mult
 ADD = mybir.AluOpType.add
+IDENTITY = mybir.ActivationFunctionType.Identity
 
 P = 128
 PACK = 4
@@ -30,8 +31,8 @@ CHUNKS = (
     (0, 0, 512, ((0, 0), (0, 0), (0, 0)), PAIR),
     (1, 0, 512, ((0, 0), (512, 0), (0, 0)), EACH),
     (2, 0, 512, ((0, 0), (512, 0), (0, 0)), EACH),
-    (3, 0, 256, ((0, 0), (0, 0), (0, 0)), EACH),
-    (3, 256, 256, ((0, 0), (0, 0), (128, 0)), EACH),
+    (3, 0, 256, ((0, 0), (256, 0), (0, 0)), EACH),
+    (3, 256, 256, ((256, 0), (0, 0), (128, 0)), EACH),
 )
 RAW_BUFS = {512: 12, 256: 6}
 GROUPED_BUFS = {1024: 1, 512: 5, 256: 3}
@@ -149,6 +150,12 @@ def tile_routed_moe_kernel(tc, xT, w, b, gate, offs, pos1, pos2, out):
                 y[i][:, pair * 2 * C:(pair + 1) * 2 * C].rearrange("p (e c) -> p e c", e=2), accs[pair, i][:],
                 bias[:, i, 2 * pair:2 * pair + 2].unsqueeze(2).to_broadcast([P, 2, C]), ADD)
 
+        def empty_on_scalar(pair, i):
+            for r in range(2):
+                e = 2 * pair + r
+                nc.scalar.activation(
+                    y[i][:, e * C:(e + 1) * C], accs[pair, i][:, r, :], IDENTITY, bias=bias[:, i, e:e + 1])
+
         def combine(i):
             first = stage.tile([P, T], F32, name="first", bufs=2)
             second = stage.tile([P, T], F32, name="second", bufs=2)
@@ -165,9 +172,8 @@ def tile_routed_moe_kernel(tc, xT, w, b, gate, offs, pos1, pos2, out):
                 nc.scalar.copy(result[:], total)
             nc.sync.dma_start(out[i * P:(i + 1) * P, :], result[:])
 
-        w_raw += [load_w(chunk) for chunk in CHUNKS[1:4]]
+        w_raw += [load_w(chunk) for chunk in CHUNKS[1:]]
         load_gates(0)
-        w_raw += [load_w(chunk) for chunk in CHUNKS[4:]]
         load_gates(1)
         for position, chunk in enumerate(CHUNKS):
             run_chunk(chunk, w_raw[position])
@@ -178,8 +184,8 @@ def tile_routed_moe_kernel(tc, xT, w, b, gate, offs, pos1, pos2, out):
                 empty(1, 0)
                 empty(1, 1)
                 combine(0)
+        empty_on_scalar(1, 2)
+        empty_on_scalar(1, 3)
         combine(1)
-        empty(1, 2)
-        empty(1, 3)
         combine(2)
         combine(3)

from contextlib import ExitStack

import concourse.mybir as mybir
from concourse.masks import make_identity

K, T, E, C, N = 1536, 512, 4, 256, 512
FLOPS = 2 * K * N * E * C

F32 = mybir.dt.float32
BF16 = mybir.dt.bfloat16
U32 = mybir.dt.uint32
U16 = mybir.dt.uint16
U8 = mybir.dt.uint8
FP8X4 = mybir.dt.float8_e4m3fn_x4
MULT = mybir.AluOpType.mult
ADD = mybir.AluOpType.add
IDENTITY = mybir.ActivationFunctionType.Identity

P = 128
PACK = 4
K_PASS = P * PACK
PASSES = K // K_PASS
SLOTS = E * C
BLOCKS = N // P
GATHER_CUTS = ((0, 384), (384, 768), (768, 1024))
X_VECTOR = (320, 0, 0)

PAIR = ((0, 1), (2,))
EACH = ((0,), (1,), (2,))
CHUNKS = (
    (0, 0, 512, ((0, 0), (0, 0), (0, 0)), PAIR),
    (1, 0, 512, ((0, 0), (512, 0), (0, 0)), EACH),
    (2, 0, 512, ((0, 0), (512, 0), (0, 0)), EACH),
    (3, 0, 256, ((0, 0), (256, 0), (0, 0)), EACH),
    (3, 256, 256, ((256, 0), (0, 0), (128, 0)), EACH),
)
RAW_BUFS = {512: 12, 256: 6}
GROUPED_BUFS = {1024: 1, 512: 5, 256: 3}
CODES_BUFS = {1024: 1, 512: 4, 256: 4}


def tile_routed_moe_kernel(tc, xT, w, b, gate, offs, pos1, pos2, out):
    nc = tc.nc
    with ExitStack() as ctx:
        keep = ctx.enter_context(tc.tile_pool(name="keep", bufs=1))
        stage = ctx.enter_context(tc.tile_pool(name="stage", bufs=2))
        psum = ctx.enter_context(tc.psum_pool(name="psum", bufs=8))

        offs_sb = keep.tile([P, SLOTS // 16], U16, name="offs_sb")
        pos1_sb = keep.tile([P, T // 16], U16, name="pos1_sb")
        pos2_sb = keep.tile([P, T // 16], U16, name="pos2_sb")
        bias = keep.tile([P, BLOCKS, E], F32, name="bias")
        x_scales = keep.tile([P, T], U8, name="x_scales", align_bytes=64)
        g_scales = keep.tile([P, SLOTS], U8, name="g_scales", align_bytes=64)
        y = [keep.tile([P, SLOTS], F32, name="y%d" % i) for i in range(BLOCKS)]
        gates = [keep.tile([P, 2, 2, T], F32, name="gates%d" % i) for i in range(2)]
        ident = keep.tile([P, P], F32, name="ident")

        nc.gpsimd.memset(x_scales[:], 0)
        make_identity(nc, ident[:])

        x_raw = []
        for g in range(PASSES):
            raw = stage.tile([P, PACK, 512], F32, name="raw512", bufs=RAW_BUFS[512])
            nc.sync.dma_start(raw[:], xT[g * K_PASS:(g + 1) * K_PASS, :].rearrange("(p j) t -> p j t", j=PACK))
            x_raw.append(raw)
            if g == 0:
                nc.sync.dma_start(offs_sb[:], offs)
        nc.scalar.dma_start(bias[:], b.rearrange("(c p) e -> p c e", p=P))

        def load_w(chunk):
            e, c0, width = chunk[:3]
            raws = []
            for g in range(PASSES):
                raw = stage.tile([P, PACK, width], F32, name="raw%d" % width, bufs=RAW_BUFS[width])
                nc.sync.dma_start(
                    raw[:], w[e, g * K_PASS:(g + 1) * K_PASS, c0:c0 + width].rearrange("(p j) n -> p j n", j=PACK))
                raws.append(raw)
            return raws

        def load_gates(h):
            for k in range(2):
                nc.sync.dma_start(
                    gates[h][:, k, :, :], gate[k, h * 256:(h + 1) * 256, :].rearrange("(c p) t -> p c t", p=P))

        def interleave(dst, raw, width, on_vector, on_gpsimd):
            first = width - on_vector - on_gpsimd
            second = width - on_gpsimd
            for copy, c0, c1 in ((nc.scalar.copy, 0, first), (nc.vector.tensor_copy, first, second)):
                if c1 > c0:
                    copy(
                        dst[:, c0:c1, :].rearrange("p (c i) j -> p c j i", i=4),
                        raw[:, :, c0:c1].rearrange("p j (c i) -> p c j i", i=4))
            if on_gpsimd > 0:
                nc.gpsimd.tensor_scalar(
                    dst[:, second:width, :].rearrange("p (c i) j -> p c j i", i=4),
                    raw[:, :, second:width].rearrange("p j (c i) -> p c j i", i=4), 1.0, 0.0, MULT, ADD)

        w_raw = [load_w(CHUNKS[0])]
        nc.sync.dma_start(pos1_sb[:], pos1)
        nc.sync.dma_start(pos2_sb[:], pos2)

        x_codes = []
        g_codes = []
        for g in range(PASSES):
            grouped = stage.tile([P, T, PACK], BF16, name="w_grouped512", bufs=GROUPED_BUFS[512], align_bytes=64)
            interleave(grouped, x_raw[g], T, X_VECTOR[g], 0)
            codes = keep.tile([P, T], U32, name="x_codes%d" % g, align_bytes=64)
            nc.vector.quantize_mx(
                out=codes[:].bitcast(FP8X4), scales=x_scales[4 * g:P, :],
                in_=grouped[:].rearrange("p t j -> p (t j)"))
            x_codes.append(codes)
            g_codes.append(keep.tile([P, SLOTS], U32, name="g_codes%d" % g, align_bytes=64))
            for s0, s1 in GATHER_CUTS:
                nc.vector.tensor_copy(g_codes[g][:, s0:s1], x_codes[g][:].indirect(offs_sb[:, s0 // 16:s1 // 16]))
        for s0, s1 in GATHER_CUTS:
            nc.vector.tensor_copy(g_scales[:, s0:s1], x_scales[:].indirect(offs_sb[:, s0 // 16:s1 // 16]))

        accs = {}

        def run_chunk(chunk, raws):
            e, c0, width, shares, groups = chunk
            blocks = range(c0 // P, (c0 + width) // P)
            slots = slice(e * C, (e + 1) * C)
            for group in groups:
                columns = len(group) * width
                grouped = stage.tile(
                    [P, columns, PACK], BF16, name="w_grouped%d" % columns, bufs=GROUPED_BUFS[columns], align_bytes=64)
                codes = stage.tile(
                    [P, columns], U32, name="w_codes%d" % columns, bufs=CODES_BUFS[columns], align_bytes=64)
                scales = stage.tile(
                    [P, columns], U8, name="w_scales%d" % columns, bufs=CODES_BUFS[columns], align_bytes=64)
                for r, g in enumerate(group):
                    interleave(grouped[:, r * width:(r + 1) * width, :], raws[g], width, shares[g][0], shares[g][1])
                nc.vector.quantize_mx(
                    out=codes[:].bitcast(FP8X4), scales=scales[:], in_=grouped[:].rearrange("p n j -> p (n j)"))
                for r, g in enumerate(group):
                    for i in blocks:
                        if g == 0 and e % 2 == 0:
                            accs[e // 2, i] = psum.tile([P, 2, C], F32, name="acc")
                        n0 = r * width + i * P - c0
                        nc.tensor.matmul_mx(
                            out=accs[e // 2, i][:, e % 2, :],
                            lhsT=codes[:, n0:n0 + P].bitcast(FP8X4), lhsT_scale=scales[:, n0:n0 + P],
                            rhs=g_codes[g][:, slots].bitcast(FP8X4), rhs_scale=g_scales[4 * g:P, slots],
                            start=(g == 0), stop=(g == PASSES - 1))

        def empty(pair, i):
            nc.vector.tensor_tensor(
                y[i][:, pair * 2 * C:(pair + 1) * 2 * C].rearrange("p (e c) -> p e c", e=2), accs[pair, i][:],
                bias[:, i, 2 * pair:2 * pair + 2].unsqueeze(2).to_broadcast([P, 2, C]), ADD)

        def empty_on_scalar(pair, i):
            for r in range(2):
                e = 2 * pair + r
                nc.scalar.activation(
                    y[i][:, e * C:(e + 1) * C], accs[pair, i][:, r, :], IDENTITY, bias=bias[:, i, e:e + 1])

        def combine(i):
            first = stage.tile([P, T], F32, name="first", bufs=2)
            second = stage.tile([P, T], F32, name="second", bufs=2)
            nc.vector.tensor_tensor(first[:], y[i][:].indirect(pos1_sb[:]), gates[i // 2][:, 0, i % 2, :], MULT)
            nc.vector.tensor_tensor(second[:], y[i][:].indirect(pos2_sb[:]), gates[i // 2][:, 1, i % 2, :], MULT)
            result = stage.tile([P, T], F32, name="result", bufs=2)
            if i == BLOCKS - 1:
                nc.vector.tensor_tensor(result[:], first[:], second[:], ADD)
            else:
                acc = psum.tile([P, 2, C], F32, name="acc")
                total = acc[:].rearrange("p e c -> p (e c)")
                nc.tensor.matmul(total, ident[:], first[:], start=True, stop=False)
                nc.tensor.matmul(total, ident[:], second[:], start=False, stop=True)
                nc.scalar.copy(result[:], total)
            nc.sync.dma_start(out[i * P:(i + 1) * P, :], result[:])

        w_raw += [load_w(chunk) for chunk in CHUNKS[1:]]
        load_gates(0)
        load_gates(1)
        for position, chunk in enumerate(CHUNKS):
            run_chunk(chunk, w_raw[position])
            if position == 2:
                for i in range(BLOCKS):
                    empty(0, i)
            if position == 3:
                empty(1, 0)
                empty(1, 1)
                combine(0)
        empty_on_scalar(1, 2)
        empty_on_scalar(1, 3)
        combine(1)
        combine(2)
        combine(3)
